import numpy as np
import ml_dtypes


def mxq(x, axis, fmt="e4m3"):
    dtype, down = {"e4m3": (ml_dtypes.float8_e4m3fn, 7), "e5m2": (ml_dtypes.float8_e5m2, 14)}[fmt]
    v = np.moveaxis(np.asarray(x, np.float32).astype(ml_dtypes.bfloat16).astype(np.float64), axis, -1)
    blocks = v.reshape(v.shape[:-1] + (-1, 32))
    amax = np.abs(blocks).max(-1, keepdims=True)
    byte = np.maximum(np.where(amax > 0, np.frexp(amax)[1] - 1 + 127, 0) - down, 1)
    scale = np.exp2(byte - 127.0)
    codes = (blocks / scale).astype(np.float32).astype(dtype).astype(np.float64)
    return np.moveaxis((codes * scale).reshape(v.shape), -1, axis)


WIDE = False


def mx_kscale(k):
    if not WIDE:
        return np.ones(k)
    levels = np.array([10, -10, 5, -5, 0])
    if k % 512:
        return np.exp2(np.random.permutation(np.resize(levels, k // 32))).repeat(32)
    a = np.empty((k // 512, 16))
    for p in range(k // 512):
        a[p, :8] = np.random.permutation(np.resize(levels, 8))
        for g in range(8):
            far = levels[np.abs(levels - a[p, g]) >= 10]
            a[p, g + 8] = far[np.random.randint(len(far))]
    return np.exp2(a.ravel()).repeat(32)


def f64(x):
    return np.asarray(x).astype(np.float64)


def striped(idx):
    return np.tile(idx.reshape(-1, 16).T, (8, 1)).astype(np.uint16)


def unstriped(offs):
    return offs[:16].T.reshape(-1).astype(np.int64)


E2M1 = np.array([0.0, 0.5, 1.0, 1.5, 2.0, 3.0, 4.0, 6.0, -0.0, -0.5, -1.0, -1.5, -2.0, -3.0, -4.0, -6.0])


def pack_weight(w, fmt):
    k, n = w.shape
    w = f64(np.asarray(w, np.float32).astype(ml_dtypes.bfloat16)).reshape(k // 32, 32, n)
    amax = np.abs(w).max(1)
    if fmt == "e4m3":
        byte = np.frexp(amax)[1] - 1 + 127 - 7
    else:
        mant, ex = np.frexp(amax / 6.0)
        byte = np.where(mant > 0.5, ex, ex - 1) + 127
    byte = np.clip(np.where(amax > 0, byte, 1), 1, 254)
    scaled = (w * np.exp2(127.0 - byte)[:, None, :]).reshape(k, n).astype(np.float32)
    by_word = np.ascontiguousarray(scaled.reshape(k // 512, 128, 4, n).transpose(0, 1, 3, 2))
    if fmt == "e4m3":
        words = by_word.astype(ml_dtypes.float8_e4m3fn).view(np.uint8)
    else:
        c = by_word.astype(ml_dtypes.float4_e2m1fn).view(np.uint8) & 0xF
        words = (c[..., 0::2] | (c[..., 1::2] << 4)).reshape(k // 512, 128, 2 * n)
    return np.ascontiguousarray(words), np.ascontiguousarray(byte.astype(np.uint8).reshape(k // 512, 16, n))


def unpack_weight(words, scales, fmt):
    g, _, n = scales.shape
    words = np.ascontiguousarray(words).reshape(g, 128, n, -1)
    if fmt == "e4m3":
        vals = words.view(ml_dtypes.float8_e4m3fn).astype(np.float64)
    else:
        nib = np.empty((g, 128, n, 4), np.uint8)
        nib[..., 0::2] = words & 0xF
        nib[..., 1::2] = words >> 4
        vals = E2M1[nib]
    vals = vals * np.repeat(np.exp2(scales.astype(np.float64) - 127.0), 8, axis=1)[..., None]
    return vals.transpose(0, 1, 3, 2).reshape(g * 512, n)


def gelu(v):
    return 0.5 * v * (1.0 + np.tanh(np.sqrt(2.0 / np.pi) * (v + 0.044715 * v**3)))


K, H, T, S, T2, P = 1024, 512, 2048, 512, 1024, 512

def setup_inputs():
    n = np.random.standard_normal
    s = mx_kscale(K)[:, None]
    u = mx_kscale(H)[:, None]
    tab_words, tab_scales = pack_weight(n((K, T)) * s, "e4m3")
    w4_words, w4_scales = pack_weight(2.0 * n((K, H)) / np.sqrt(K) / s * u.T, "e2m1")
    w1 = (n((K, H)) / np.sqrt(K) / s).astype(np.float32)
    w2 = (0.55 * n((K, H)) / np.sqrt(K) / s).astype(np.float32)
    page0 = (0.8 * n((H, T2)) * u).astype(np.float32)
    wgs = np.exp(0.3 * n((128, S))).astype(np.float32)
    gain = (np.random.uniform(0.5, 1.5, H) / np.sqrt(H) / u[:, 0] ** 2).astype(np.float32)
    flux = (0.8 * n(P)).astype(np.float32)
    offs = striped(np.random.permutation(T)[:S])
    offs2 = striped(np.random.permutation(T2)[:S])
    offs3 = striped(np.random.permutation(T2)[:P])
    offs4 = striped(np.random.permutation(T2)[:P])
    return {"tab_words": tab_words, "tab_scales": tab_scales, "offs": offs,
            "w1": w1, "w2": w2, "w4_words": w4_words, "w4_scales": w4_scales,
            "page0": page0, "wgs": wgs, "offs2": offs2, "offs3": offs3,
            "offs4": offs4, "gain": gain, "flux": flux}

def reference(tab_words, tab_scales, offs, w1, w2, w4_words, w4_scales,
              page0, wgs, offs2, offs3, offs4, gain, flux):
    v = unpack_weight(tab_words, tab_scales, "e4m3")[:, unstriped(offs)]
    w4 = unpack_weight(w4_words, w4_scales, "e2m1")
    b = np.tanh(mxq(f64(w1), 0, "e4m3").T @ v)
    d = np.sin(mxq(f64(w2), 0, "e4m3").T @ v)
    h = (b + d) * (w4.T @ v)
    page = f64(page0).copy()
    page[:, unstriped(offs2)] = np.tile(f64(wgs), (H // 128, 1)) * h
    x1 = page[:, unstriped(offs3)]
    x2 = np.abs(page[:, unstriped(offs4)]) * f64(gain)[:, None]
    e = mxq(x1, 0, "e4m3").T @ mxq(x2, 0, "e4m3")
    return e + f64(flux)[None, :]

@@ -1,0 +1,350 @@
+from contextlib import ExitStack
+
+import concourse.mybir as mybir
+from concourse.masks import make_identity
+
+K, H, T, S, T2, NP = 1024, 512, 2048, 512, 1024, 512
+FLOPS = 2 * (3 * K * H * S + H * NP * NP)
+
+F32 = mybir.dt.float32
+BF16 = mybir.dt.bfloat16
+I32 = mybir.dt.int32
+U32 = mybir.dt.uint32
+U16 = mybir.dt.uint16
+U8 = mybir.dt.uint8
+FP8X4 = mybir.dt.float8_e4m3fn_x4
+FP4X4 = mybir.dt.float4_e2m1fn_x4
+ACT = mybir.ActivationFunctionType
+ALU = mybir.AluOpType
+
+P = 128
+PASSES = 2
+HALF = H // 2
+
+
+def tile_list_steel_flux_reactivity_kernel(
+    tc, tab_words, tab_scales, offs, w1, w2, w4_words, w4_scales,
+    page0, wgs, offs2, offs3, offs4, gain, flux, out,
+):
+    nc = tc.nc
+    with ExitStack() as ctx:
+        sb = ctx.enter_context(tc.tile_pool(name="sb", bufs=1))
+        shared = ctx.enter_context(tc.tile_pool(name="shared", bufs=1))
+        ps = ctx.enter_context(tc.psum_pool(name="ps", bufs=2))
+
+        def tile(shape, dtype, name, tag=None):
+            return sb.tile(shape, dtype, name=name, tag=tag or name, align_bytes=64)
+
+        def placed(shape, dtype, name, offset):
+            return shared.tile(shape, dtype, name=name, offset=offset, align_bytes=64)
+
+        LATE = 4 * (S + 2 * 2 * S) + 2 * 4 * P
+        TAIL = LATE + 3072
+        lists = [sb.tile([P, S // 16], U16, name="list%d" % i) for i in range(4)]
+        tab_w = [tile([P, T], I32, "tab_w%d" % a) for a in range(PASSES)]
+        tab_s = tile([P, PASSES, T], U8, "tab_s")
+        w4_w = tile([P, PASSES, 2 * H], U8, "w4_w")
+        w4_s = tile([P, PASSES, H], U8, "w4_s")
+        raw = {}
+        for i in range(2):
+            for a in range(PASSES):
+                for hf in range(2):
+                    if (i, a, hf) == (1, 1, 1):
+                        raw[i, a, hf] = placed([P, 4, HALF], F32, "raw111", LATE - 1024)
+                    else:
+                        raw[i, a, hf] = tile([P, 4, HALF], F32, "raw%d%d%d" % (i, a, hf))
+        page = [tile([P, T2], F32, "page%d" % t) for t in range(4)]
+        wg_even = tile([P, S], F32, "wg_even")
+        wg_odd = tile([P, 2, S], F32, "wg_odd")
+        gain_even = tile([P, 2, 2], F32, "gain_even")
+        gain_all = tile([P, 4], F32, "gain_all")
+        flux_rows = tile([P, NP], F32, "flux_rows")
+        ident = tile([P, P], F32, "ident")
+
+        nc.vector.memset(tab_s[:].bitcast(I32), 0)
+        nc.gpsimd.memset(w4_s[:].bitcast(I32), 0)
+
+        def load_w(i, a, hf):
+            src = (w1, w2)[i][a * 512:(a + 1) * 512, hf * HALF:(hf + 1) * HALF]
+            nc.sync.dma_start(out=raw[i, a, hf][:], in_=src.rearrange("(p j) c -> p j c", j=4))
+
+        def load_table(a):
+            nc.sync.dma_start(out=tab_w[a][:], in_=tab_words[a].rearrange("p t i -> p (t i)").bitcast(I32))
+
+        def load_scales(queue, dst, src):
+            for q in range(4):
+                queue.dma_start(
+                    out=dst[32 * q:32 * q + 4].bitcast(I32),
+                    in_=src[:, 4 * q:4 * q + 4, :].rearrange("a r t -> r a t").bitcast(I32))
+
+        page_rows = [page0[0:HALF:2, :], page0[HALF:H:2, :], page0[1:H:4, :], page0[3:H:4, :]]
+
+        nc.sync.dma_start(lists[0][:], offs)
+        load_table(0)
+        load_scales(nc.sync, tab_s, tab_scales)
+        load_table(1)
+        make_identity(nc, ident[:])
+        load_w(0, 0, 0)
+        nc.sync.dma_start(out=w4_w[:], in_=w4_words.rearrange("a p n -> p a n"))
+        load_scales(nc.sync, w4_s, w4_scales)
+        load_w(0, 1, 0)
+        load_w(1, 0, 0)
+        load_w(1, 1, 0)
+        nc.sync.dma_start(lists[1][:], offs2)
+        for hf in range(2):
+            nc.sync.dma_start(out=wg_even[64 * hf:64 * hf + 64, :], in_=wgs[0:P:2, :])
+        nc.sync.dma_start(out=page[0][:], in_=page_rows[0])
+        for i in range(2):
+            for a in range(PASSES):
+                load_w(i, a, 1)
+        nc.sync.dma_start(lists[3][:], offs4)
+        nc.sync.dma_start(lists[2][:], offs3)
+        nc.sync.dma_start(out=gain_even[:], in_=gain.rearrange("(h p e) -> p h e", h=2, e=2))
+        nc.sync.dma_start(out=gain_all[:], in_=gain.rearrange("(p t) -> p t", t=4))
+        for t in range(1, 4):
+            nc.sync.dma_start(out=page[t][:], in_=page_rows[t])
+        for q in range(4):
+            nc.sync.dma_start(
+                out=wg_odd[32 * q:32 * q + 32],
+                in_=wgs[1:P:2, :].rearrange("(m u) j -> m u j", u=2))
+        nc.sync.dma_start(out=flux_rows[:], in_=flux.partition_broadcast(P))
+
+        v_w = [tile([P, S], U32, "v_w%d" % a) for a in range(PASSES)]
+        v_s = [tile([P, S], U8, "v_s%d" % a) for a in range(PASSES)]
+        for a in range(PASSES):
+            nc.vector.tensor_copy(v_w[a][:], tab_w[a][:].bitcast(U32).indirect(lists[0][:]))
+            nc.vector.tensor_copy(v_s[a][:], tab_s[:, a, :].indirect(lists[0][:]))
+
+        w4_wd = [tile([P, PASSES, H], U8, "w4_wd%d" % o) for o in range(2)]
+        w4_sd = [tile([P, PASSES, HALF], U8, "w4_sd%d" % o) for o in range(2)]
+
+        def deal_w4(o):
+            for src, dst in ((w4_w[:].bitcast(U16), w4_wd[o][:].bitcast(U16)), (w4_s[:], w4_sd[o][:])):
+                if o == 0:
+                    nc.vector.tensor_copy(dst, src[:, :, 0:H:2])
+                else:
+                    nc.vector.tensor_copy(
+                        dst.rearrange("p a (u m) -> p a u m", u=2),
+                        src[:, :, 1:H:2].rearrange("p a (m u) -> p a u m", u=2))
+
+        w_c, w_s = {}, {}
+        HELD = [(0, 0, 1), (0, 1, 1), (1, 0, 1), (1, 1, 1)]
+        for i in range(2):
+            for hf in range(2):
+                for o in range(2):
+                    w_c[i, hf, o] = tile([P, PASSES * P], U32, "w_c%d%d%d" % (i, hf, o))
+                    if (i, hf, o) not in HELD:
+                        w_s[i, hf, o] = tile([P, PASSES * P], U8, "w_s%d%d%d" % (i, hf, o))
+
+        def quantise(codes, scales, values):
+            nc.vector.quantize_mx(out=codes.bitcast(FP8X4), scales=scales, in_=values)
+
+        def cast(i, a, hf, o, stage, copy=nc.scalar.copy):
+            copy(stage.rearrange("p (m j) -> p m j", j=4),
+                 raw[i, a, hf][:, :, o:HALF:2].rearrange("p j m -> p m j"))
+
+        def cast_pass(i, a, hf, o, stage, copy=nc.scalar.copy):
+            cast(i, a, hf, o, stage, copy)
+            cols = slice(P * a, P * (a + 1))
+            quantise(w_c[i, hf, o][:, cols], w_s[i, hf, o][:, cols], stage)
+
+        def cast_both(i, hf, o, stage):
+            for a in range(PASSES):
+                cast(i, a, hf, o, stage[:, 4 * P * a:4 * P * (a + 1)])
+            quantise(w_c[i, hf, o][:], w_s[i, hf, o][:], stage)
+
+        wg = [wg_even[:], wg_even[:], wg_odd[:, 0, :], wg_odd[:, 1, :]]
+        gain_col = [gain_even[:, 0, 0:1], gain_even[:, 1, 0:1], gain_all[:, 1:2], gain_all[:, 3:4]]
+
+        def transposed_part(i, hf, o, part, j0=0, j1=S):
+            bank = ps.tile([P, 4, P], F32, name="pre", bufs=4)
+            for a in range(PASSES):
+                cols = slice(P * a, P * (a + 1))
+                for j in range(j0, j1, P):
+                    nc.tensor.matmul_mx(
+                        out=bank[:, (j - j0) // P, :],
+                        lhsT=v_w[a][:, j:j + P].bitcast(FP8X4), lhsT_scale=v_s[a][:, j:j + P],
+                        rhs=w_c[i, hf, o][:, cols].bitcast(FP8X4), rhs_scale=w_s[i, hf, o][:, cols],
+                        start=(a == 0 and j == j0), stop=(a == PASSES - 1 and j == j1 - P))
+            nc.scalar.activation(part, bank[:, 0:(j1 - j0) // P, :], (ACT.Tanh, ACT.Sin)[i])
+
+        def direct_sum(i, t, j0, j1):
+            bank = ps.tile([P, 4, P], F32, name="pre", bufs=4)
+            flat = bank[:].rearrange("p b r -> p (b r)")[:, 0:j1 - j0]
+            for a in range(PASSES):
+                cols = slice(P * a, P * (a + 1))
+                nc.tensor.matmul_mx(
+                    out=flat, lhsT=w_c[i, t, 0][:, cols].bitcast(FP8X4), lhsT_scale=w_s[i, t, 0][:, cols],
+                    rhs=v_w[a][:, j0:j1].bitcast(FP8X4), rhs_scale=v_s[a][:, j0:j1],
+                    start=(a == 0), stop=(a == PASSES - 1))
+            return flat
+
+        def third_sum(t):
+            third = ps.tile([P, S], F32, name="third", tag=("bank_a", "bank_b")[t == 3], bufs=1)
+            for a in range(PASSES):
+                nc.tensor.matmul_mx(
+                    out=third[:], lhsT=w4_wd[t // 2][:, a, 2 * P * (t % 2):2 * P * (t % 2 + 1)].bitcast(FP4X4),
+                    lhsT_scale=w4_sd[t // 2][:, a, P * (t % 2):P * (t % 2 + 1)],
+                    rhs=v_w[a][:].bitcast(FP8X4), rhs_scale=v_s[a][:],
+                    start=(a == 0), stop=(a == PASSES - 1))
+            return third
+
+        def scatter(t, h, j0, j1):
+            nc.vector.tensor_tensor(page[t][:].indirect(lists[1][:, j0 // 16:j1 // 16]), h[:], wg[t][:, j0:j1], ALU.mult)
+
+        def put_direct(t, saturating, third):
+            halves = [slice(0, 256), slice(256, S)]
+            periodic = tile([P, S], F32, "sin%d" % t)
+            total = tile([P, S], F32, "sum%d" % t)
+            h = tile([P, S], F32, "h%d" % t)
+            for js in halves:
+                nc.scalar.activation(periodic[:, js], direct_sum(1, t, js.start, js.stop), ACT.Sin)
+            for js in halves:
+                nc.vector.tensor_tensor(total[:, js], saturating[:, js], periodic[:, js], ALU.add)
+            for js in halves:
+                nc.vector.tensor_tensor(h[:, js], total[:, js], third[:, js], ALU.mult)
+            scatter(t, h, 0, S)
+
+        def third_copy(t, tag=None):
+            strength = tile([P, S], F32, "strength%d" % t, tag)
+            nc.scalar.copy(strength[:], third_sum(t)[:])
+            return strength
+
+        def put(t, saturating, periodic, strength, j0=0, j1=S):
+            blocks = (j1 - j0) // P
+            total = ps.tile([P, S], F32, name="total", tag=("bank_b", "bank_a")[t == 3], bufs=1)
+            for i, part in enumerate((saturating, periodic)):
+                for b in range(blocks):
+                    nc.tensor.matmul(total[:, P * b:P * (b + 1)], part[:, b, :], ident[:], is_transpose=True,
+                                     start=(i == 0 and b == 0), stop=(i == 1 and b == blocks - 1))
+            h = placed([P, S], F32, "h3", TAIL + 5120) if t == 3 else tile([P, S], F32, "h2")
+            nc.vector.tensor_tensor(h[:], total[:, 0:j1 - j0], strength[:, j0:j1], ALU.mult)
+            return h
+
+        x1_moved = tile([P, 2, NP], BF16, "x1_moved")
+
+        def move(dst, src, t):
+            for e in range(2):
+                nc.sync.dma_start(out=dst[64 * t:64 * t + 64, e, :], in_=src[e:P:2, :])
+
+        def flux_pick(t, c0, c1, tag=None):
+            picked = tile([P, c1 - c0], F32, "picked%d_%d" % (t, c0), tag)
+            nc.vector.tensor_copy(picked[:], page[t][:].indirect(lists[3][:, c0 // 16:c1 // 16]))
+            return picked
+
+        def flux_scale(t, picked, dst, size):
+            nc.scalar.activation(size[:], picked[:], ACT.Abs)
+            for part, lo, hi in dst:
+                nc.scalar.activation(part, size[:, lo:hi], ACT.Copy, scale=gain_col[t])
+
+        def steel_pick(t, plane):
+            nc.vector.tensor_copy(plane[:], page[t][:].indirect(lists[2][:]))
+            move(x1_moved, plane, t)
+
+        def flux_move(t, picked, tag):
+            plane = tile([P, NP], BF16, "plane2_%d" % t)
+            flux_scale(t, picked, [(plane[:], 0, NP)], tile([P, NP], F32, "size%d" % t, tag))
+            move(x2_moved, plane, t)
+
+        x2_moved = placed([P, 2, NP], BF16, "x2_moved", TAIL + 3072)
+        deal_w4(0)
+        for i in range(2):
+            for a in range(PASSES):
+                stage = tile([P, 4 * P], BF16, "even%d%d0" % (i, a))
+                cast_pass(i, a, 0, 0, stage[:], (nc.scalar.copy, nc.vector.tensor_copy)[i])
+        saturating = tile([P, S], F32, "tanh0")
+        nc.scalar.activation(saturating[:], direct_sum(0, 0, 0, S), ACT.Tanh)
+        third = third_sum(0)
+        put_direct(0, saturating, third)
+        cast_both(0, 1, 0, tile([P, 8 * P], BF16, "even01")[:])
+        picked0 = flux_pick(0, 0, NP, "raw011")
+        cast_both(1, 1, 0, tile([P, 8 * P], BF16, "even11")[:])
+        steel_pick(0, placed([P, NP], BF16, "plane1_0", LATE + 1024))
+        for n, key in enumerate(HELD):
+            w_s[key] = placed([P, PASSES * P], U8, "w_s%d%d%d" % key, LATE + 256 * n)
+        late = placed([P, LATE // 4], F32, "late", 0)
+        saturating = late[:, 0:S]
+        odd_parts = [late[:, (1 + 2 * i) * S:(3 + 2 * i) * S].rearrange("p (b r) -> p b r", b=4) for i in range(2)]
+        late_stage = late[:, 5 * S:5 * S + 256].bitcast(BF16)
+        nc.scalar.activation(saturating, direct_sum(0, 1, 0, S), ACT.Tanh)
+        cast_pass(1, 0, 0, 1, tile([P, 4 * P], BF16, "odd100")[:])
+        cast_pass(1, 1, 0, 1, late_stage)
+        put_direct(1, saturating, third_sum(1))
+        deal_w4(1)
+        for hf in range(2):
+            cast_both(0, hf, 1, tile([P, 8 * P], BF16, "odd0%d" % hf)[:])
+        cast_both(1, 1, 1, tile([P, 8 * P], BF16, "odd11")[:])
+        picked1 = flux_pick(1, 0, NP)
+        steel_pick(1, tile([P, NP], BF16, "plane1_1"))
+        strength = third_copy(2, "sin1")
+        flux_move(0, picked0, "sum1")
+        for i in range(2):
+            for hf in range(2):
+                transposed_part(i, hf, 1, odd_parts[i][:, :, P * hf:P * (hf + 1)])
+        scatter(2, put(2, odd_parts[0][:, :, 0:HALF:2], odd_parts[1][:, :, 0:HALF:2], strength), 0, S)
+        flux_move(1, picked1, "w_c111")
+        x2_g = [placed([P, 256, 4], BF16, "x2_g0", TAIL), tile([P, 256, 4], BF16, "x2_g1")]
+        h = put(3, odd_parts[0][:, :, 1:HALF:2], odd_parts[1][:, :, 1:HALF:2], third_copy(3))
+        picked2 = tile([P, NP], F32, "picked2")
+        nc.vector.tensor_copy(picked2[:], page[2][:].indirect(lists[3][:]))
+        scatter(3, h, 0, S)
+        picked3 = [flux_pick(3, 256 * c, 256 * (c + 1)) for c in range(2)]
+        for c in range(2):
+            nc.scalar.copy(x2_g[c][:, :, 0:2], x2_moved[:, :, 256 * c:256 * (c + 1)].rearrange("p e j -> p j e"))
+        flux_scale(2, picked2, [(x2_g[c][:, :, 2], 256 * c, 256 * (c + 1)) for c in range(2)],
+                   placed([P, NP], F32, "size2", TAIL + 3072))
+        pieces = [(0, 256), (256, 384), (384, 512)]
+        x1_g = []
+
+        def steels_moved(n, offset):
+            m0, m1 = pieces[n]
+            x1_g.append(placed([P, m1 - m0, 4], BF16, "x1_g%d" % n, offset))
+            nc.scalar.copy(x1_g[n][:, :, 0:2], x1_moved[:, :, m0:m1].rearrange("p e m -> p m e"))
+
+        steels_moved(0, TAIL + 4096)
+        size = placed([P, NP], F32, "size3", TAIL + 2048)
+        for c in range(2):
+            cols = slice(256 * c, 256 * (c + 1))
+            nc.scalar.activation(size[:, cols], picked3[c][:], ACT.Abs)
+            nc.scalar.activation(x2_g[c][:, :, 3], size[:, cols], ACT.Copy, scale=gain_col[3])
+
+        x2_c = tile([P, NP], U32, "x2_c")
+        x2_s = tile([P, NP], U8, "x2_s")
+        x1_c = tile([P, NP], U32, "x1_c")
+        x1_s = tile([P, NP], U8, "x1_s")
+
+        def steels(n):
+            m0, m1 = pieces[n]
+            for t in (2, 3):
+                nc.vector.tensor_copy(x1_g[n][:, :, t], page[t][:].indirect(lists[2][:, m0 // 16:m1 // 16]))
+            quantise(x1_c[:, m0:m1], x1_s[:, m0:m1], x1_g[n][:].rearrange("p m s -> p (m s)"))
+
+        def score(q):
+            cols = slice(P * q, P * (q + 1))
+            bank = ps.tile([P, NP], F32, name="score", tag="pre", bufs=4)
+            for c in range(2):
+                half = slice(256 * c, 256 * (c + 1))
+                nc.tensor.matmul_mx(
+                    out=bank[:, half], lhsT=x1_c[:, cols].bitcast(FP8X4), lhsT_scale=x1_s[:, cols],
+                    rhs=x2_c[:, half].bitcast(FP8X4), rhs_scale=x2_s[:, half], start=True, stop=True)
+            res = tile([P, NP], F32, "res%d" % q)
+            if q == 0:
+                sums = tile([P, NP], F32, "sums")
+                nc.scalar.copy(sums[:], bank[:])
+                nc.gpsimd.tensor_tensor(res[:], sums[:], flux_rows[:], ALU.add)
+            else:
+                nc.vector.tensor_tensor(res[:], bank[:], flux_rows[:], ALU.add)
+            nc.sync.dma_start(out=out[cols, :], in_=res[:])
+
+        def flux_quantise(c):
+            cols = slice(256 * c, 256 * (c + 1))
+            quantise(x2_c[:, cols], x2_s[:, cols], x2_g[c][:].rearrange("p j s -> p (j s)"))
+
+        steels(0)
+        for c in range(2):
+            flux_quantise(c)
+        for n in (1, 2):
+            steels_moved(n, TAIL + 1024 * (n - 1))
+            steels(n)
+        for q in range(4):
+            score(q)

@@ -61,6 +61,10 @@ def tile_list_steel_flux_reactivity_kernel(
         flux_rows = tile([P, NP], F32, "flux_rows")
         ident = tile([P, P], F32, "ident")
 
+        warm = tile([P, 2], F32, "warm")
+        nc.gpsimd.memset(warm[:, 0:1], 0.0)
+        nc.scalar.activation(warm[:, 1:2], warm[:, 0:1], ACT.Silu)
+
         nc.vector.memset(tab_s[:].bitcast(I32), 0)
         nc.gpsimd.memset(w4_s[:].bitcast(I32), 0)
 

@@ -38,7 +38,7 @@ def tile_list_steel_flux_reactivity_kernel(
         def placed(shape, dtype, name, offset):
             return shared.tile(shape, dtype, name=name, offset=offset, align_bytes=64)
 
-        LATE = 4 * (S + 2 * 2 * S) + 2 * 4 * P
+        LATE = 4 * (S + 2 * 2 * S)
         TAIL = LATE + 3072
         lists = [sb.tile([P, S // 16], U16, name="list%d" % i) for i in range(4)]
         tab_w = [tile([P, T], I32, "tab_w%d" % a) for a in range(PASSES)]
@@ -58,7 +58,7 @@ def tile_list_steel_flux_reactivity_kernel(
         wg_odd = tile([P, 2, S], F32, "wg_odd")
         gain_even = tile([P, 2, 2], F32, "gain_even")
         gain_all = tile([P, 4], F32, "gain_all")
-        flux_rows = tile([P, NP], F32, "flux_rows")
+        flux_cols = tile([P, 4], F32, "flux_cols")
         ident = tile([P, P], F32, "ident")
 
         warm = tile([P, 2], F32, "warm")
@@ -105,13 +105,14 @@ def tile_list_steel_flux_reactivity_kernel(
         nc.sync.dma_start(lists[2][:], offs3)
         nc.sync.dma_start(out=gain_even[:], in_=gain.rearrange("(h p e) -> p h e", h=2, e=2))
         nc.sync.dma_start(out=gain_all[:], in_=gain.rearrange("(p t) -> p t", t=4))
-        for t in range(1, 4):
+        nc.sync.dma_start(out=flux_cols[:], in_=flux.rearrange("(p b) -> p b", b=4))
+        for t in range(1, 3):
             nc.sync.dma_start(out=page[t][:], in_=page_rows[t])
         for q in range(4):
             nc.sync.dma_start(
                 out=wg_odd[32 * q:32 * q + 32],
                 in_=wgs[1:P:2, :].rearrange("(m u) j -> m u j", u=2))
-        nc.sync.dma_start(out=flux_rows[:], in_=flux.partition_broadcast(P))
+        nc.sync.dma_start(out=page[3][:], in_=page_rows[3])
 
         v_w = [tile([P, S], U32, "v_w%d" % a) for a in range(PASSES)]
         v_s = [tile([P, S], U8, "v_s%d" % a) for a in range(PASSES)]
@@ -143,19 +144,23 @@ def tile_list_steel_flux_reactivity_kernel(
         def quantise(codes, scales, values):
             nc.vector.quantize_mx(out=codes.bitcast(FP8X4), scales=scales, in_=values)
 
-        def cast(i, a, hf, o, stage, copy=nc.scalar.copy):
-            copy(stage.rearrange("p (m j) -> p m j", j=4),
-                 raw[i, a, hf][:, :, o:HALF:2].rearrange("p j m -> p m j"))
+        def cast_parity(i, a, hf, o, stage):
+            nc.vector.tensor_copy(stage.rearrange("p (c n j) -> p c j n", n=2, j=4),
+                                  raw[i, a, hf][:, :, o:HALF:2].rearrange("p j (c n) -> p c j n", n=2))
 
-        def cast_pass(i, a, hf, o, stage, copy=nc.scalar.copy):
-            cast(i, a, hf, o, stage, copy)
+        def cast_load(i, a, hf, stage):
+            nc.scalar.copy(stage.rearrange("p o (c n j) -> p c j n o", n=2, j=4),
+                           raw[i, a, hf][:].rearrange("p j (c n o) -> p c j n o", n=2, o=2))
+
+        def quantise_pass(i, a, hf, o, stage):
             cols = slice(P * a, P * (a + 1))
             quantise(w_c[i, hf, o][:, cols], w_s[i, hf, o][:, cols], stage)
 
-        def cast_both(i, hf, o, stage):
+        def cast_second_half(i):
+            stage = tile([P, 2, PASSES, 4 * P], BF16, "stage%d1" % i)
             for a in range(PASSES):
-                cast(i, a, hf, o, stage[:, 4 * P * a:4 * P * (a + 1)])
-            quantise(w_c[i, hf, o][:], w_s[i, hf, o][:], stage)
+                cast_load(i, a, 1, stage[:, :, a, :])
+            return [stage[:, o].rearrange("p a c -> p (a c)") for o in range(2)]
 
         wg = [wg_even[:], wg_even[:], wg_odd[:, 0, :], wg_odd[:, 1, :]]
         gain_col = [gain_even[:, 0, 0:1], gain_even[:, 1, 0:1], gain_all[:, 1:2], gain_all[:, 3:4]]
@@ -170,7 +175,7 @@ def tile_list_steel_flux_reactivity_kernel(
                         lhsT=v_w[a][:, j:j + P].bitcast(FP8X4), lhsT_scale=v_s[a][:, j:j + P],
                         rhs=w_c[i, hf, o][:, cols].bitcast(FP8X4), rhs_scale=w_s[i, hf, o][:, cols],
                         start=(a == 0 and j == j0), stop=(a == PASSES - 1 and j == j1 - P))
-            nc.scalar.activation(part, bank[:, 0:(j1 - j0) // P, :], (ACT.Tanh, ACT.Sin)[i])
+            nc.scalar.activation(part, bank[:].rearrange("p b (m u) -> p b u m", u=2), (ACT.Tanh, ACT.Sin)[i])
 
         def direct_sum(i, t, j0, j1):
             bank = ps.tile([P, 4, P], F32, name="pre", bufs=4)
@@ -252,43 +257,57 @@ def tile_list_steel_flux_reactivity_kernel(
 
         x2_moved = placed([P, 2, NP], BF16, "x2_moved", TAIL + 3072)
         deal_w4(0)
-        for i in range(2):
-            for a in range(PASSES):
-                stage = tile([P, 4 * P], BF16, "even%d%d0" % (i, a))
-                cast_pass(i, a, 0, 0, stage[:], (nc.scalar.copy, nc.vector.tensor_copy)[i])
+        first = [tile([P, 2, 4 * P], BF16, "stage0%d0" % a) for a in range(PASSES)]
+        for a in range(PASSES):
+            cast_load(0, a, 0, first[a][:])
+            quantise_pass(0, a, 0, 0, first[a][:, 0, :])
+        for a in range(PASSES):
+            stage = tile([P, 4 * P], BF16, "even1%d0" % a)
+            cast_parity(1, a, 0, 0, stage[:])
+            quantise_pass(1, a, 0, 0, stage[:])
+        odd10 = tile([P, PASSES * 4 * P], BF16, "odd10", "even110")
+        for a in range(PASSES):
+            cast_parity(1, a, 0, 1, odd10[:, 4 * P * a:4 * P * (a + 1)])
         saturating = tile([P, S], F32, "tanh0")
         nc.scalar.activation(saturating[:], direct_sum(0, 0, 0, S), ACT.Tanh)
         third = third_sum(0)
         put_direct(0, saturating, third)
-        cast_both(0, 1, 0, tile([P, 8 * P], BF16, "even01")[:])
+        second = [cast_second_half(0)]
+        quantise(w_c[0, 1, 0][:], w_s[0, 1, 0][:], second[0][0])
         picked0 = flux_pick(0, 0, NP, "raw011")
-        cast_both(1, 1, 0, tile([P, 8 * P], BF16, "even11")[:])
+        second.append(cast_second_half(1))
+        quantise(w_c[1, 1, 0][:], w_s[1, 1, 0][:], second[1][0])
         steel_pick(0, placed([P, NP], BF16, "plane1_0", LATE + 1024))
         for n, key in enumerate(HELD):
             w_s[key] = placed([P, PASSES * P], U8, "w_s%d%d%d" % key, LATE + 256 * n)
         late = placed([P, LATE // 4], F32, "late", 0)
         saturating = late[:, 0:S]
-        odd_parts = [late[:, (1 + 2 * i) * S:(3 + 2 * i) * S].rearrange("p (b r) -> p b r", b=4) for i in range(2)]
-        late_stage = late[:, 5 * S:5 * S + 256].bitcast(BF16)
+        odd_parts = [late[:, (1 + 2 * i) * S:(3 + 2 * i) * S].rearrange("p (b u r) -> p b u r", b=4, u=2) for i in range(2)]
         nc.scalar.activation(saturating, direct_sum(0, 1, 0, S), ACT.Tanh)
-        cast_pass(1, 0, 0, 1, tile([P, 4 * P], BF16, "odd100")[:])
-        cast_pass(1, 1, 0, 1, late_stage)
+        for a in range(PASSES):
+            quantise_pass(0, a, 0, 1, first[a][:, 1, :])
+        quantise(w_c[0, 1, 1][:], w_s[0, 1, 1][:], second[0][1])
+        quantise(w_c[1, 0, 1][:], w_s[1, 0, 1][:], odd10[:])
+        quantise(w_c[1, 1, 1][:], w_s[1, 1, 1][:], second[1][1])
         put_direct(1, saturating, third_sum(1))
         deal_w4(1)
-        for hf in range(2):
-            cast_both(0, hf, 1, tile([P, 8 * P], BF16, "odd0%d" % hf)[:])
-        cast_both(1, 1, 1, tile([P, 8 * P], BF16, "odd11")[:])
         picked1 = flux_pick(1, 0, NP)
         steel_pick(1, tile([P, NP], BF16, "plane1_1"))
         strength = third_copy(2, "sin1")
         flux_move(0, picked0, "sum1")
         for i in range(2):
             for hf in range(2):
-                transposed_part(i, hf, 1, odd_parts[i][:, :, P * hf:P * (hf + 1)])
-        scatter(2, put(2, odd_parts[0][:, :, 0:HALF:2], odd_parts[1][:, :, 0:HALF:2], strength), 0, S)
+                transposed_part(i, hf, 1, odd_parts[i][:, :, :, 64 * hf:64 * (hf + 1)])
+        scatter(2, put(2, odd_parts[0][:, :, 0, :], odd_parts[1][:, :, 0, :], strength), 0, S)
         flux_move(1, picked1, "w_c111")
         x2_g = [placed([P, 256, 4], BF16, "x2_g0", TAIL), tile([P, 256, 4], BF16, "x2_g1")]
-        h = put(3, odd_parts[0][:, :, 1:HALF:2], odd_parts[1][:, :, 1:HALF:2], third_copy(3))
+        h = put(3, odd_parts[0][:, :, 1, :], odd_parts[1][:, :, 1, :], third_copy(3))
+        spread = ps.tile([P, 4, P], F32, name="spread", tag="bank_b", bufs=1)
+        for b in range(4):
+            nc.tensor.matmul(spread[:, b, :], flux_cols[:, b:b + 1].to_broadcast([P, P]), ident[:],
+                             is_transpose=True, start=True, stop=True)
+        flux_rows = tile([P, NP], F32, "flux_rows")
+        nc.scalar.copy(flux_rows[:].rearrange("m (p b) -> m p b", b=4), spread[:].rearrange("m b p -> m p b"))
         picked2 = tile([P, NP], F32, "picked2")
         nc.vector.tensor_copy(picked2[:], page[2][:].indirect(lists[3][:]))
         scatter(3, h, 0, S)
@@ -332,12 +351,7 @@ def tile_list_steel_flux_reactivity_kernel(
                     out=bank[:, half], lhsT=x1_c[:, cols].bitcast(FP8X4), lhsT_scale=x1_s[:, cols],
                     rhs=x2_c[:, half].bitcast(FP8X4), rhs_scale=x2_s[:, half], start=True, stop=True)
             res = tile([P, NP], F32, "res%d" % q)
-            if q == 0:
-                sums = tile([P, NP], F32, "sums")
-                nc.scalar.copy(sums[:], bank[:])
-                nc.gpsimd.tensor_tensor(res[:], sums[:], flux_rows[:], ALU.add)
-            else:
-                nc.vector.tensor_tensor(res[:], bank[:], flux_rows[:], ALU.add)
+            nc.vector.tensor_tensor(res[:], bank[:], flux_rows[:], ALU.add)
             nc.sync.dma_start(out=out[cols, :], in_=res[:])
 
         def flux_quantise(c):

@@ -42,7 +42,7 @@ def tile_list_steel_flux_reactivity_kernel(
         TAIL = LATE + 3072
         lists = [sb.tile([P, S // 16], U16, name="list%d" % i) for i in range(4)]
         tab_w = [tile([P, T], I32, "tab_w%d" % a) for a in range(PASSES)]
-        tab_s = tile([P, PASSES, T], U8, "tab_s")
+        tab_s = tile([P, T], U8, "tab_s")
         w4_w = tile([P, PASSES, 2 * H], U8, "w4_w")
         w4_s = tile([P, PASSES, H], U8, "w4_s")
         raw = {}
@@ -85,24 +85,28 @@ def tile_list_steel_flux_reactivity_kernel(
 
         nc.sync.dma_start(lists[0][:], offs)
         load_table(0)
-        load_scales(nc.sync, tab_s, tab_scales)
+        for q in range(4):
+            nc.sync.dma_start(out=tab_s[32 * q:32 * q + 8].bitcast(I32),
+                              in_=tab_scales[:, 4 * q:4 * q + 4, :].bitcast(I32))
         load_table(1)
+        v_s1 = tile([P, S], U8, "v_s1")
+        nc.gpsimd.memset(v_s1[:].bitcast(I32), 0)
+        load_scales(nc.gpsimd, w4_s, w4_scales)
         make_identity(nc, ident[:])
         load_w(0, 0, 0)
-        nc.sync.dma_start(out=w4_w[:], in_=w4_words.rearrange("a p n -> p a n"))
-        load_scales(nc.sync, w4_s, w4_scales)
         load_w(0, 1, 0)
         load_w(1, 0, 0)
         load_w(1, 1, 0)
+        nc.sync.dma_start(out=w4_w[:], in_=w4_words.rearrange("a p n -> p a n"))
         nc.sync.dma_start(lists[1][:], offs2)
         for hf in range(2):
             nc.sync.dma_start(out=wg_even[64 * hf:64 * hf + 64, :], in_=wgs[0:P:2, :])
         nc.sync.dma_start(out=page[0][:], in_=page_rows[0])
+        nc.sync.dma_start(lists[3][:], offs4)
+        nc.sync.dma_start(lists[2][:], offs3)
         for i in range(2):
             for a in range(PASSES):
                 load_w(i, a, 1)
-        nc.sync.dma_start(lists[3][:], offs4)
-        nc.sync.dma_start(lists[2][:], offs3)
         nc.sync.dma_start(out=gain_even[:], in_=gain.rearrange("(h p e) -> p h e", h=2, e=2))
         nc.sync.dma_start(out=gain_all[:], in_=gain.rearrange("(p t) -> p t", t=4))
         nc.sync.dma_start(out=flux_cols[:], in_=flux.rearrange("(p b) -> p b", b=4))
@@ -115,15 +119,20 @@ def tile_list_steel_flux_reactivity_kernel(
         nc.sync.dma_start(out=page[3][:], in_=page_rows[3])
 
         v_w = [tile([P, S], U32, "v_w%d" % a) for a in range(PASSES)]
-        v_s = [tile([P, S], U8, "v_s%d" % a) for a in range(PASSES)]
-        for a in range(PASSES):
-            nc.vector.tensor_copy(v_w[a][:], tab_w[a][:].bitcast(U32).indirect(lists[0][:]))
-            nc.vector.tensor_copy(v_s[a][:], tab_s[:, a, :].indirect(lists[0][:]))
+        v_packed = tile([P, S], U8, "v_packed")
+        v_s = [v_packed[4 * a:P] for a in range(PASSES)]
+        nc.vector.tensor_copy(v_w[0][:], tab_w[0][:].bitcast(U32).indirect(lists[0][:]))
+        nc.vector.tensor_copy(v_packed[:], tab_s[:].indirect(lists[0][:]))
+        nc.vector.tensor_copy(v_w[1][:], tab_w[1][:].bitcast(U32).indirect(lists[0][:]))
+        for q in range(4):
+            nc.gpsimd.dma_start(out=v_s1[32 * q:32 * q + 4].bitcast(I32),
+                                in_=v_packed[32 * q + 4:32 * q + 8].bitcast(I32))
 
         w4_wd = [tile([P, PASSES, H], U8, "w4_wd%d" % o) for o in range(2)]
-        w4_sd = [tile([P, PASSES, HALF], U8, "w4_sd%d" % o) for o in range(2)]
+        w4_sd = []
 
-        def deal_w4(o):
+        def deal_w4(o, tag):
+            w4_sd.append(tile([P, PASSES, HALF], U8, "w4_sd%d" % o, tag))
             for src, dst in ((w4_w[:].bitcast(U16), w4_wd[o][:].bitcast(U16)), (w4_s[:], w4_sd[o][:])):
                 if o == 0:
                     nc.vector.tensor_copy(dst, src[:, :, 0:H:2])
@@ -133,13 +142,10 @@ def tile_list_steel_flux_reactivity_kernel(
                         src[:, :, 1:H:2].rearrange("p a (m u) -> p a u m", u=2))
 
         w_c, w_s = {}, {}
-        HELD = [(0, 0, 1), (0, 1, 1), (1, 0, 1), (1, 1, 1)]
         for i in range(2):
             for hf in range(2):
-                for o in range(2):
-                    w_c[i, hf, o] = tile([P, PASSES * P], U32, "w_c%d%d%d" % (i, hf, o))
-                    if (i, hf, o) not in HELD:
-                        w_s[i, hf, o] = tile([P, PASSES * P], U8, "w_s%d%d%d" % (i, hf, o))
+                w_c[i, hf, 0] = tile([P, PASSES * P], U32, "w_c%d%d" % (i, hf))
+                w_s[i, hf, 0] = tile([P, PASSES * P], U8, "w_s%d%d" % (i, hf))
 
         def quantise(codes, scales, values):
             nc.vector.quantize_mx(out=codes.bitcast(FP8X4), scales=scales, in_=values)
@@ -156,11 +162,13 @@ def tile_list_steel_flux_reactivity_kernel(
             cols = slice(P * a, P * (a + 1))
             quantise(w_c[i, hf, o][:, cols], w_s[i, hf, o][:, cols], stage)
 
-        def cast_second_half(i):
-            stage = tile([P, 2, PASSES, 4 * P], BF16, "stage%d1" % i)
-            for a in range(PASSES):
-                cast_load(i, a, 1, stage[:, :, a, :])
-            return [stage[:, o].rearrange("p a c -> p (a c)") for o in range(2)]
+        def quantise_odd(i, stage, order):
+            codes = tile([P, 4 * P], U32, "odd_c%d" % i)
+            scales = placed([P, 4 * P], U8, "odd_s%d" % i, LATE + 512 * i)
+            quantise(codes[:], scales[:], stage)
+            for n, hf in enumerate(order):
+                w_c[i, hf, 1] = codes[:, HALF * n:HALF * (n + 1)]
+                w_s[i, hf, 1] = scales[:, HALF * n:HALF * (n + 1)]
 
         wg = [wg_even[:], wg_even[:], wg_odd[:, 0, :], wg_odd[:, 1, :]]
         gain_col = [gain_even[:, 0, 0:1], gain_even[:, 1, 0:1], gain_all[:, 1:2], gain_all[:, 3:4]]
@@ -194,7 +202,7 @@ def tile_list_steel_flux_reactivity_kernel(
                 nc.tensor.matmul_mx(
                     out=third[:], lhsT=w4_wd[t // 2][:, a, 2 * P * (t % 2):2 * P * (t % 2 + 1)].bitcast(FP4X4),
                     lhsT_scale=w4_sd[t // 2][:, a, P * (t % 2):P * (t % 2 + 1)],
-                    rhs=v_w[a][:].bitcast(FP8X4), rhs_scale=v_s[a][:],
+                    rhs=v_w[a][:].bitcast(FP8X4), rhs_scale=(v_packed, v_s1)[a][:],
                     start=(a == 0), stop=(a == PASSES - 1))
             return third
 
@@ -256,41 +264,40 @@ def tile_list_steel_flux_reactivity_kernel(
             move(x2_moved, plane, t)
 
         x2_moved = placed([P, 2, NP], BF16, "x2_moved", TAIL + 3072)
-        deal_w4(0)
-        first = [tile([P, 2, 4 * P], BF16, "stage0%d0" % a) for a in range(PASSES)]
+        RUN = PASSES * 4 * P
+        stage1 = tile([P, 4 * RUN], BF16, "stage1")
+        by_load = stage1[:].rearrange("p (o h a c) -> p h a o c", o=2, h=2, a=PASSES)
         for a in range(PASSES):
-            cast_load(0, a, 0, first[a][:])
-            quantise_pass(0, a, 0, 0, first[a][:, 0, :])
+            cast_load(0, a, 0, by_load[:, 0, a])
+            quantise_pass(0, a, 0, 0, stage1[:, 4 * P * a:4 * P * (a + 1)])
         for a in range(PASSES):
             stage = tile([P, 4 * P], BF16, "even1%d0" % a)
             cast_parity(1, a, 0, 0, stage[:])
             quantise_pass(1, a, 0, 0, stage[:])
-        odd10 = tile([P, PASSES * 4 * P], BF16, "odd10", "even110")
+        deal_w4(0, "raw000")
+        stage2 = tile([P, 3 * RUN], BF16, "stage2", "even110")
         for a in range(PASSES):
-            cast_parity(1, a, 0, 1, odd10[:, 4 * P * a:4 * P * (a + 1)])
+            cast_parity(1, a, 0, 1, stage2[:, 2 * RUN + 4 * P * a:2 * RUN + 4 * P * (a + 1)])
         saturating = tile([P, S], F32, "tanh0")
         nc.scalar.activation(saturating[:], direct_sum(0, 0, 0, S), ACT.Tanh)
         third = third_sum(0)
         put_direct(0, saturating, third)
-        second = [cast_second_half(0)]
-        quantise(w_c[0, 1, 0][:], w_s[0, 1, 0][:], second[0][0])
+        for a in range(PASSES):
+            cast_load(0, a, 1, by_load[:, 1, a])
+        quantise(w_c[0, 1, 0][:], w_s[0, 1, 0][:], stage1[:, RUN:2 * RUN])
         picked0 = flux_pick(0, 0, NP, "raw011")
-        second.append(cast_second_half(1))
-        quantise(w_c[1, 1, 0][:], w_s[1, 1, 0][:], second[1][0])
-        steel_pick(0, placed([P, NP], BF16, "plane1_0", LATE + 1024))
-        for n, key in enumerate(HELD):
-            w_s[key] = placed([P, PASSES * P], U8, "w_s%d%d%d" % key, LATE + 256 * n)
+        for a in range(PASSES):
+            cast_load(1, a, 1, stage2[:, 0:2 * RUN].rearrange("p (o a c) -> p a o c", o=2, a=PASSES)[:, a])
+        quantise(w_c[1, 1, 0][:], w_s[1, 1, 0][:], stage2[:, 0:RUN])
+        steel_pick(0, tile([P, NP], BF16, "plane1_0", "raw101"))
         late = placed([P, LATE // 4], F32, "late", 0)
         saturating = late[:, 0:S]
         odd_parts = [late[:, (1 + 2 * i) * S:(3 + 2 * i) * S].rearrange("p (b u r) -> p b u r", b=4, u=2) for i in range(2)]
         nc.scalar.activation(saturating, direct_sum(0, 1, 0, S), ACT.Tanh)
-        for a in range(PASSES):
-            quantise_pass(0, a, 0, 1, first[a][:, 1, :])
-        quantise(w_c[0, 1, 1][:], w_s[0, 1, 1][:], second[0][1])
-        quantise(w_c[1, 0, 1][:], w_s[1, 0, 1][:], odd10[:])
-        quantise(w_c[1, 1, 1][:], w_s[1, 1, 1][:], second[1][1])
+        quantise_odd(0, stage1[:, 2 * RUN:4 * RUN], (0, 1))
+        quantise_odd(1, stage2[:, RUN:3 * RUN], (1, 0))
         put_direct(1, saturating, third_sum(1))
-        deal_w4(1)
+        deal_w4(1, "raw010")
         picked1 = flux_pick(1, 0, NP)
         steel_pick(1, tile([P, NP], BF16, "plane1_1"))
         strength = third_copy(2, "sin1")
@@ -299,7 +306,7 @@ def tile_list_steel_flux_reactivity_kernel(
             for hf in range(2):
                 transposed_part(i, hf, 1, odd_parts[i][:, :, :, 64 * hf:64 * (hf + 1)])
         scatter(2, put(2, odd_parts[0][:, :, 0, :], odd_parts[1][:, :, 0, :], strength), 0, S)
-        flux_move(1, picked1, "w_c111")
+        flux_move(1, picked1, "odd_c1")
         x2_g = [placed([P, 256, 4], BF16, "x2_g0", TAIL), tile([P, 256, 4], BF16, "x2_g1")]
         h = put(3, odd_parts[0][:, :, 1, :], odd_parts[1][:, :, 1, :], third_copy(3))
         spread = ps.tile([P, 4, P], F32, name="spread", tag="bank_b", bufs=1)

@@ -40,6 +40,7 @@ def tile_list_steel_flux_reactivity_kernel(
 
         LATE = 4 * (S + 2 * 2 * S)
         TAIL = LATE + 3072
+        HOLD = TAIL + 7168
         lists = [sb.tile([P, S // 16], U16, name="list%d" % i) for i in range(4)]
         tab_w = [tile([P, T], I32, "tab_w%d" % a) for a in range(PASSES)]
         tab_s = tile([P, T], U8, "tab_s")
@@ -83,8 +84,8 @@ def tile_list_steel_flux_reactivity_kernel(
 
         page_rows = [page0[0:HALF:2, :], page0[HALF:H:2, :], page0[1:H:4, :], page0[3:H:4, :]]
 
-        nc.sync.dma_start(lists[0][:], offs)
         load_table(0)
+        nc.sync.dma_start(lists[0][:], offs)
         for q in range(4):
             nc.sync.dma_start(out=tab_s[32 * q:32 * q + 8].bitcast(I32),
                               in_=tab_scales[:, 4 * q:4 * q + 4, :].bitcast(I32))
@@ -99,20 +100,21 @@ def tile_list_steel_flux_reactivity_kernel(
         load_w(1, 1, 0)
         nc.sync.dma_start(out=w4_w[:], in_=w4_words.rearrange("a p n -> p a n"))
         nc.sync.dma_start(lists[1][:], offs2)
-        for hf in range(2):
-            nc.sync.dma_start(out=wg_even[64 * hf:64 * hf + 64, :], in_=wgs[0:P:2, :])
+        for q in (0, 2, 1, 3):
+            nc.sync.dma_start(out=wg_even[32 * q:32 * q + 32, :], in_=wgs[64 * (q % 2):64 * (q % 2 + 1):2, :])
         nc.sync.dma_start(out=page[0][:], in_=page_rows[0])
+        load_w(0, 0, 1)
         nc.sync.dma_start(lists[3][:], offs4)
         nc.sync.dma_start(lists[2][:], offs3)
-        for i in range(2):
-            for a in range(PASSES):
-                load_w(i, a, 1)
+        load_w(0, 1, 1)
+        load_w(1, 0, 1)
+        load_w(1, 1, 1)
         nc.sync.dma_start(out=gain_even[:], in_=gain.rearrange("(h p e) -> p h e", h=2, e=2))
         nc.sync.dma_start(out=gain_all[:], in_=gain.rearrange("(p t) -> p t", t=4))
         nc.sync.dma_start(out=flux_cols[:], in_=flux.rearrange("(p b) -> p b", b=4))
         for t in range(1, 3):
             nc.sync.dma_start(out=page[t][:], in_=page_rows[t])
-        for q in range(4):
+        for q in (0, 2, 1, 3):
             nc.sync.dma_start(
                 out=wg_odd[32 * q:32 * q + 32],
                 in_=wgs[1:P:2, :].rearrange("(m u) j -> m u j", u=2))
@@ -145,14 +147,14 @@ def tile_list_steel_flux_reactivity_kernel(
         for i in range(2):
             for hf in range(2):
                 w_c[i, hf, 0] = tile([P, PASSES * P], U32, "w_c%d%d" % (i, hf))
-                w_s[i, hf, 0] = tile([P, PASSES * P], U8, "w_s%d%d" % (i, hf))
+            w_s[i, 0, 0] = tile([P, PASSES * P], U8, "w_s%d0" % i)
 
         def quantise(codes, scales, values):
             nc.vector.quantize_mx(out=codes.bitcast(FP8X4), scales=scales, in_=values)
 
-        def cast_parity(i, a, hf, o, stage):
-            nc.vector.tensor_copy(stage.rearrange("p (c n j) -> p c j n", n=2, j=4),
-                                  raw[i, a, hf][:, :, o:HALF:2].rearrange("p j (c n) -> p c j n", n=2))
+        def cast_parity(copy, i, a, hf, o, stage):
+            copy(stage.rearrange("p (c n j) -> p c j n", n=2, j=4),
+                 raw[i, a, hf][:, :, o:HALF:2].rearrange("p j (c n) -> p c j n", n=2))
 
         def cast_load(i, a, hf, stage):
             nc.scalar.copy(stage.rearrange("p o (c n j) -> p c j n o", n=2, j=4),
@@ -163,7 +165,7 @@ def tile_list_steel_flux_reactivity_kernel(
             quantise(w_c[i, hf, o][:, cols], w_s[i, hf, o][:, cols], stage)
 
         def quantise_odd(i, stage, order):
-            codes = tile([P, 4 * P], U32, "odd_c%d" % i)
+            codes = placed([P, 4 * P], U32, "odd_c%d" % i, HOLD + 2560 * i)
             scales = placed([P, 4 * P], U8, "odd_s%d" % i, LATE + 512 * i)
             quantise(codes[:], scales[:], stage)
             for n, hf in enumerate(order):
@@ -197,7 +199,7 @@ def tile_list_steel_flux_reactivity_kernel(
             return flat
 
         def third_sum(t):
-            third = ps.tile([P, S], F32, name="third", tag=("bank_a", "bank_b")[t == 3], bufs=1)
+            third = ps.tile([P, S], F32, name="third", tag="bank_a", bufs=1)
             for a in range(PASSES):
                 nc.tensor.matmul_mx(
                     out=third[:], lhsT=w4_wd[t // 2][:, a, 2 * P * (t % 2):2 * P * (t % 2 + 1)].bitcast(FP4X4),
@@ -213,7 +215,7 @@ def tile_list_steel_flux_reactivity_kernel(
             halves = [slice(0, 256), slice(256, S)]
             periodic = tile([P, S], F32, "sin%d" % t)
             total = tile([P, S], F32, "sum%d" % t)
-            h = tile([P, S], F32, "h%d" % t)
+            h = placed([P, S], F32, "h0", HOLD + 1536) if t == 0 else tile([P, S], F32, "h1")
             for js in halves:
                 nc.scalar.activation(periodic[:, js], direct_sum(1, t, js.start, js.stop), ACT.Sin)
             for js in halves:
@@ -229,7 +231,7 @@ def tile_list_steel_flux_reactivity_kernel(
 
         def put(t, saturating, periodic, strength, j0=0, j1=S):
             blocks = (j1 - j0) // P
-            total = ps.tile([P, S], F32, name="total", tag=("bank_b", "bank_a")[t == 3], bufs=1)
+            total = ps.tile([P, S], F32, name="total", tag="bank_b", bufs=1)
             for i, part in enumerate((saturating, periodic)):
                 for b in range(blocks):
                     nc.tensor.matmul(total[:, P * b:P * (b + 1)], part[:, b, :], ident[:], is_transpose=True,
@@ -240,9 +242,9 @@ def tile_list_steel_flux_reactivity_kernel(
 
         x1_moved = tile([P, 2, NP], BF16, "x1_moved")
 
-        def move(dst, src, t):
+        def move(queue, dst, src, t):
             for e in range(2):
-                nc.sync.dma_start(out=dst[64 * t:64 * t + 64, e, :], in_=src[e:P:2, :])
+                queue.dma_start(out=dst[64 * t:64 * t + 64, e, :], in_=src[e:P:2, :])
 
         def flux_pick(t, c0, c1, tag=None):
             picked = tile([P, c1 - c0], F32, "picked%d_%d" % (t, c0), tag)
@@ -256,12 +258,12 @@ def tile_list_steel_flux_reactivity_kernel(
 
         def steel_pick(t, plane):
             nc.vector.tensor_copy(plane[:], page[t][:].indirect(lists[2][:]))
-            move(x1_moved, plane, t)
+            move(nc.sync, x1_moved, plane, t)
 
-        def flux_move(t, picked, tag):
+        def flux_move(t, picked, size):
             plane = tile([P, NP], BF16, "plane2_%d" % t)
-            flux_scale(t, picked, [(plane[:], 0, NP)], tile([P, NP], F32, "size%d" % t, tag))
-            move(x2_moved, plane, t)
+            flux_scale(t, picked, [(plane[:], 0, NP)], size)
+            move(nc.scalar, x2_moved, plane, t)
 
         x2_moved = placed([P, 2, NP], BF16, "x2_moved", TAIL + 3072)
         RUN = PASSES * 4 * P
@@ -272,24 +274,28 @@ def tile_list_steel_flux_reactivity_kernel(
             quantise_pass(0, a, 0, 0, stage1[:, 4 * P * a:4 * P * (a + 1)])
         for a in range(PASSES):
             stage = tile([P, 4 * P], BF16, "even1%d0" % a)
-            cast_parity(1, a, 0, 0, stage[:])
+            cast_parity(nc.vector.tensor_copy, 1, a, 0, 0, stage[:])
             quantise_pass(1, a, 0, 0, stage[:])
         deal_w4(0, "raw000")
-        stage2 = tile([P, 3 * RUN], BF16, "stage2", "even110")
-        for a in range(PASSES):
-            cast_parity(1, a, 0, 1, stage2[:, 2 * RUN + 4 * P * a:2 * RUN + 4 * P * (a + 1)])
         saturating = tile([P, S], F32, "tanh0")
         nc.scalar.activation(saturating[:], direct_sum(0, 0, 0, S), ACT.Tanh)
         third = third_sum(0)
         put_direct(0, saturating, third)
+        for i in range(2):
+            w_s[i, 1, 0] = placed([P, PASSES * P], U8, "w_s%d1" % i, HOLD + 2048 + 256 * i)
+        stage2 = tile([P, 3 * RUN], BF16, "stage2", "sin0")
+        for a in range(PASSES):
+            cast_parity(nc.scalar.copy, 1, a, 0, 1, stage2[:, 2 * RUN + 4 * P * a:2 * RUN + 4 * P * (a + 1)])
         for a in range(PASSES):
             cast_load(0, a, 1, by_load[:, 1, a])
         quantise(w_c[0, 1, 0][:], w_s[0, 1, 0][:], stage1[:, RUN:2 * RUN])
         picked0 = flux_pick(0, 0, NP, "raw011")
-        for a in range(PASSES):
-            cast_load(1, a, 1, stage2[:, 0:2 * RUN].rearrange("p (o a c) -> p a o c", o=2, a=PASSES)[:, a])
-        quantise(w_c[1, 1, 0][:], w_s[1, 1, 0][:], stage2[:, 0:RUN])
+        cast_load(1, 0, 1, stage2[:, 0:2 * RUN].rearrange("p (o a c) -> p a o c", o=2, a=PASSES)[:, 0])
         steel_pick(0, tile([P, NP], BF16, "plane1_0", "raw101"))
+        quantise_pass(1, 0, 1, 0, stage2[:, 0:4 * P])
+        for o in range(2):
+            cast_parity(nc.scalar.copy, 1, 1, 1, o, stage2[:, RUN * o + 4 * P:RUN * (o + 1)])
+        quantise_pass(1, 1, 1, 0, stage2[:, 4 * P:RUN])
         late = placed([P, LATE // 4], F32, "late", 0)
         saturating = late[:, 0:S]
         odd_parts = [late[:, (1 + 2 * i) * S:(3 + 2 * i) * S].rearrange("p (b u r) -> p b u r", b=4, u=2) for i in range(2)]
@@ -301,21 +307,21 @@ def tile_list_steel_flux_reactivity_kernel(
         picked1 = flux_pick(1, 0, NP)
         steel_pick(1, tile([P, NP], BF16, "plane1_1"))
         strength = third_copy(2, "sin1")
-        flux_move(0, picked0, "sum1")
+        flux_move(0, picked0, tile([P, NP], F32, "size0", "sum1"))
         for i in range(2):
             for hf in range(2):
                 transposed_part(i, hf, 1, odd_parts[i][:, :, :, 64 * hf:64 * (hf + 1)])
         scatter(2, put(2, odd_parts[0][:, :, 0, :], odd_parts[1][:, :, 0, :], strength), 0, S)
-        flux_move(1, picked1, "odd_c1")
+        flux_move(1, picked1, placed([P, NP], F32, "size1", HOLD + 2560))
         x2_g = [placed([P, 256, 4], BF16, "x2_g0", TAIL), tile([P, 256, 4], BF16, "x2_g1")]
         h = put(3, odd_parts[0][:, :, 1, :], odd_parts[1][:, :, 1, :], third_copy(3))
-        spread = ps.tile([P, 4, P], F32, name="spread", tag="bank_b", bufs=1)
+        spread = ps.tile([P, 4, P], F32, name="spread", tag="bank_a", bufs=1)
         for b in range(4):
             nc.tensor.matmul(spread[:, b, :], flux_cols[:, b:b + 1].to_broadcast([P, P]), ident[:],
                              is_transpose=True, start=True, stop=True)
         flux_rows = tile([P, NP], F32, "flux_rows")
         nc.scalar.copy(flux_rows[:].rearrange("m (p b) -> m p b", b=4), spread[:].rearrange("m b p -> m p b"))
-        picked2 = tile([P, NP], F32, "picked2")
+        picked2 = placed([P, NP], F32, "picked2", 0)
         nc.vector.tensor_copy(picked2[:], page[2][:].indirect(lists[3][:]))
         scatter(3, h, 0, S)
         picked3 = [flux_pick(3, 256 * c, 256 * (c + 1)) for c in range(2)]
@@ -323,7 +329,7 @@ def tile_list_steel_flux_reactivity_kernel(
             nc.scalar.copy(x2_g[c][:, :, 0:2], x2_moved[:, :, 256 * c:256 * (c + 1)].rearrange("p e j -> p j e"))
         flux_scale(2, picked2, [(x2_g[c][:, :, 2], 256 * c, 256 * (c + 1)) for c in range(2)],
                    placed([P, NP], F32, "size2", TAIL + 3072))
-        pieces = [(0, 256), (256, 384), (384, 512)]
+        pieces = [(0, 256), (256, 512)]
         x1_g = []
 
         def steels_moved(n, offset):
@@ -368,8 +374,7 @@ def tile_list_steel_flux_reactivity_kernel(
         steels(0)
         for c in range(2):
             flux_quantise(c)
-        for n in (1, 2):
-            steels_moved(n, TAIL + 1024 * (n - 1))
-            steels(n)
+        steels_moved(1, TAIL)
+        steels(1)
         for q in range(4):
             score(q)

from contextlib import ExitStack

import concourse.mybir as mybir
from concourse.masks import make_identity

K, H, T, S, T2, NP = 1024, 512, 2048, 512, 1024, 512
FLOPS = 2 * (3 * K * H * S + H * NP * NP)

F32 = mybir.dt.float32
BF16 = mybir.dt.bfloat16
I32 = mybir.dt.int32
U32 = mybir.dt.uint32
U16 = mybir.dt.uint16
U8 = mybir.dt.uint8
FP8X4 = mybir.dt.float8_e4m3fn_x4
FP4X4 = mybir.dt.float4_e2m1fn_x4
ACT = mybir.ActivationFunctionType
ALU = mybir.AluOpType

P = 128
PASSES = 2
HALF = H // 2


def tile_list_steel_flux_reactivity_kernel(
    tc, tab_words, tab_scales, offs, w1, w2, w4_words, w4_scales,
    page0, wgs, offs2, offs3, offs4, gain, flux, out,
):
    nc = tc.nc
    with ExitStack() as ctx:
        sb = ctx.enter_context(tc.tile_pool(name="sb", bufs=1))
        shared = ctx.enter_context(tc.tile_pool(name="shared", bufs=1))
        ps = ctx.enter_context(tc.psum_pool(name="ps", bufs=2))

        def tile(shape, dtype, name, tag=None):
            return sb.tile(shape, dtype, name=name, tag=tag or name, align_bytes=64)

        def placed(shape, dtype, name, offset):
            return shared.tile(shape, dtype, name=name, offset=offset, align_bytes=64)

        LATE = 4 * (S + 2 * 2 * S)
        TAIL = LATE + 3072
        HOLD = TAIL + 7168
        lists = [sb.tile([P, S // 16], U16, name="list%d" % i) for i in range(4)]
        tab_w = [tile([P, T], I32, "tab_w%d" % a) for a in range(PASSES)]
        tab_s = tile([P, T], U8, "tab_s")
        w4_w = tile([P, PASSES, 2 * H], U8, "w4_w")
        w4_s = tile([P, PASSES, H], U8, "w4_s")
        raw = {}
        for i in range(2):
            for a in range(PASSES):
                for hf in range(2):
                    if (i, a, hf) == (1, 1, 1):
                        raw[i, a, hf] = placed([P, 4, HALF], F32, "raw111", LATE - 1024)
                    else:
                        raw[i, a, hf] = tile([P, 4, HALF], F32, "raw%d%d%d" % (i, a, hf))
        page = [tile([P, T2], F32, "page%d" % t) for t in range(4)]
        wg_even = tile([P, S], F32, "wg_even")
        wg_odd = tile([P, 2, S], F32, "wg_odd")
        gain_even = tile([P, 2, 2], F32, "gain_even")
        gain_all = tile([P, 4], F32, "gain_all")
        flux_cols = tile([P, 4], F32, "flux_cols")
        ident = tile([P, P], F32, "ident")

        warm = tile([P, 2], F32, "warm")
        nc.gpsimd.memset(warm[:, 0:1], 0.0)
        nc.scalar.activation(warm[:, 1:2], warm[:, 0:1], ACT.Silu)

        nc.vector.memset(tab_s[:].bitcast(I32), 0)
        nc.gpsimd.memset(w4_s[:].bitcast(I32), 0)

        def load_w(i, a, hf):
            src = (w1, w2)[i][a * 512:(a + 1) * 512, hf * HALF:(hf + 1) * HALF]
            nc.sync.dma_start(out=raw[i, a, hf][:], in_=src.rearrange("(p j) c -> p j c", j=4))

        def load_table(a):
            nc.sync.dma_start(out=tab_w[a][:], in_=tab_words[a].rearrange("p t i -> p (t i)").bitcast(I32))

        def load_scales(queue, dst, src):
            for q in range(4):
                queue.dma_start(
                    out=dst[32 * q:32 * q + 4].bitcast(I32),
                    in_=src[:, 4 * q:4 * q + 4, :].rearrange("a r t -> r a t").bitcast(I32))

        page_rows = [page0[0:HALF:2, :], page0[HALF:H:2, :], page0[1:H:4, :], page0[3:H:4, :]]

        load_table(0)
        nc.sync.dma_start(lists[0][:], offs)
        for q in range(4):
            nc.sync.dma_start(out=tab_s[32 * q:32 * q + 8].bitcast(I32),
                              in_=tab_scales[:, 4 * q:4 * q + 4, :].bitcast(I32))
        load_table(1)
        v_s1 = tile([P, S], U8, "v_s1")
        nc.gpsimd.memset(v_s1[:].bitcast(I32), 0)
        load_scales(nc.gpsimd, w4_s, w4_scales)
        make_identity(nc, ident[:])
        load_w(0, 0, 0)
        load_w(0, 1, 0)
        load_w(1, 0, 0)
        load_w(1, 1, 0)
        nc.sync.dma_start(out=w4_w[:], in_=w4_words.rearrange("a p n -> p a n"))
        nc.sync.dma_start(lists[1][:], offs2)
        for q in (0, 2, 1, 3):
            nc.sync.dma_start(out=wg_even[32 * q:32 * q + 32, :], in_=wgs[64 * (q % 2):64 * (q % 2 + 1):2, :])
        nc.sync.dma_start(out=page[0][:], in_=page_rows[0])
        load_w(0, 0, 1)
        nc.sync.dma_start(lists[3][:], offs4)
        nc.sync.dma_start(lists[2][:], offs3)
        load_w(0, 1, 1)
        load_w(1, 0, 1)
        load_w(1, 1, 1)
        nc.sync.dma_start(out=gain_even[:], in_=gain.rearrange("(h p e) -> p h e", h=2, e=2))
        nc.sync.dma_start(out=gain_all[:], in_=gain.rearrange("(p t) -> p t", t=4))
        nc.sync.dma_start(out=flux_cols[:], in_=flux.rearrange("(p b) -> p b", b=4))
        for t in range(1, 3):
            nc.sync.dma_start(out=page[t][:], in_=page_rows[t])
        for q in (0, 2, 1, 3):
            nc.sync.dma_start(
                out=wg_odd[32 * q:32 * q + 32],
                in_=wgs[1:P:2, :].rearrange("(m u) j -> m u j", u=2))
        nc.sync.dma_start(out=page[3][:], in_=page_rows[3])

        v_w = [tile([P, S], U32, "v_w%d" % a) for a in range(PASSES)]
        v_packed = tile([P, S], U8, "v_packed")
        v_s = [v_packed[4 * a:P] for a in range(PASSES)]
        nc.vector.tensor_copy(v_w[0][:], tab_w[0][:].bitcast(U32).indirect(lists[0][:]))
        nc.vector.tensor_copy(v_packed[:], tab_s[:].indirect(lists[0][:]))
        nc.vector.tensor_copy(v_w[1][:], tab_w[1][:].bitcast(U32).indirect(lists[0][:]))
        for q in range(4):
            nc.gpsimd.dma_start(out=v_s1[32 * q:32 * q + 4].bitcast(I32),
                                in_=v_packed[32 * q + 4:32 * q + 8].bitcast(I32))

        w4_wd = [tile([P, PASSES, H], U8, "w4_wd%d" % o) for o in range(2)]
        w4_sd = []

        def deal_w4(o, tag):
            w4_sd.append(tile([P, PASSES, HALF], U8, "w4_sd%d" % o, tag))
            for src, dst in ((w4_w[:].bitcast(U16), w4_wd[o][:].bitcast(U16)), (w4_s[:], w4_sd[o][:])):
                if o == 0:
                    nc.vector.tensor_copy(dst, src[:, :, 0:H:2])
                else:
                    nc.vector.tensor_copy(
                        dst.rearrange("p a (u m) -> p a u m", u=2),
                        src[:, :, 1:H:2].rearrange("p a (m u) -> p a u m", u=2))

        w_c, w_s = {}, {}
        for i in range(2):
            for hf in range(2):
                w_c[i, hf, 0] = tile([P, PASSES * P], U32, "w_c%d%d" % (i, hf))
            w_s[i, 0, 0] = tile([P, PASSES * P], U8, "w_s%d0" % i)

        def quantise(codes, scales, values):
            nc.vector.quantize_mx(out=codes.bitcast(FP8X4), scales=scales, in_=values)

        def cast_parity(copy, i, a, hf, o, stage):
            copy(stage.rearrange("p (c n j) -> p c j n", n=2, j=4),
                 raw[i, a, hf][:, :, o:HALF:2].rearrange("p j (c n) -> p c j n", n=2))

        def cast_load(i, a, hf, stage):
            nc.scalar.copy(stage.rearrange("p o (c n j) -> p c j n o", n=2, j=4),
                           raw[i, a, hf][:].rearrange("p j (c n o) -> p c j n o", n=2, o=2))

        def quantise_pass(i, a, hf, o, stage):
            cols = slice(P * a, P * (a + 1))
            quantise(w_c[i, hf, o][:, cols], w_s[i, hf, o][:, cols], stage)

        def quantise_odd(i, stage, order):
            codes = placed([P, 4 * P], U32, "odd_c%d" % i, HOLD + 2560 * i)
            scales = placed([P, 4 * P], U8, "odd_s%d" % i, LATE + 512 * i)
            quantise(codes[:], scales[:], stage)
            for n, hf in enumerate(order):
                w_c[i, hf, 1] = codes[:, HALF * n:HALF * (n + 1)]
                w_s[i, hf, 1] = scales[:, HALF * n:HALF * (n + 1)]

        wg = [wg_even[:], wg_even[:], wg_odd[:, 0, :], wg_odd[:, 1, :]]
        gain_col = [gain_even[:, 0, 0:1], gain_even[:, 1, 0:1], gain_all[:, 1:2], gain_all[:, 3:4]]

        def transposed_part(i, hf, o, part, j0=0, j1=S):
            bank = ps.tile([P, 4, P], F32, name="pre", bufs=4)
            for a in range(PASSES):
                cols = slice(P * a, P * (a + 1))
                for j in range(j0, j1, P):
                    nc.tensor.matmul_mx(
                        out=bank[:, (j - j0) // P, :],
                        lhsT=v_w[a][:, j:j + P].bitcast(FP8X4), lhsT_scale=v_s[a][:, j:j + P],
                        rhs=w_c[i, hf, o][:, cols].bitcast(FP8X4), rhs_scale=w_s[i, hf, o][:, cols],
                        start=(a == 0 and j == j0), stop=(a == PASSES - 1 and j == j1 - P))
            nc.scalar.activation(part, bank[:].rearrange("p b (m u) -> p b u m", u=2), (ACT.Tanh, ACT.Sin)[i])

        def direct_sum(i, t, j0, j1):
            bank = ps.tile([P, 4, P], F32, name="pre", bufs=4)
            flat = bank[:].rearrange("p b r -> p (b r)")[:, 0:j1 - j0]
            for a in range(PASSES):
                cols = slice(P * a, P * (a + 1))
                nc.tensor.matmul_mx(
                    out=flat, lhsT=w_c[i, t, 0][:, cols].bitcast(FP8X4), lhsT_scale=w_s[i, t, 0][:, cols],
                    rhs=v_w[a][:, j0:j1].bitcast(FP8X4), rhs_scale=v_s[a][:, j0:j1],
                    start=(a == 0), stop=(a == PASSES - 1))
            return flat

        def third_sum(t):
            third = ps.tile([P, S], F32, name="third", tag="bank_a", bufs=1)
            for a in range(PASSES):
                nc.tensor.matmul_mx(
                    out=third[:], lhsT=w4_wd[t // 2][:, a, 2 * P * (t % 2):2 * P * (t % 2 + 1)].bitcast(FP4X4),
                    lhsT_scale=w4_sd[t // 2][:, a, P * (t % 2):P * (t % 2 + 1)],
                    rhs=v_w[a][:].bitcast(FP8X4), rhs_scale=(v_packed, v_s1)[a][:],
                    start=(a == 0), stop=(a == PASSES - 1))
            return third

        def scatter(t, h, j0, j1):
            nc.vector.tensor_tensor(page[t][:].indirect(lists[1][:, j0 // 16:j1 // 16]), h[:], wg[t][:, j0:j1], ALU.mult)

        def put_direct(t, saturating, third):
            halves = [slice(0, 256), slice(256, S)]
            periodic = tile([P, S], F32, "sin%d" % t)
            total = tile([P, S], F32, "sum%d" % t)
            h = placed([P, S], F32, "h0", HOLD + 1536) if t == 0 else tile([P, S], F32, "h1")
            for js in halves:
                nc.scalar.activation(periodic[:, js], direct_sum(1, t, js.start, js.stop), ACT.Sin)
            for js in halves:
                nc.vector.tensor_tensor(total[:, js], saturating[:, js], periodic[:, js], ALU.add)
            for js in halves:
                nc.vector.tensor_tensor(h[:, js], total[:, js], third[:, js], ALU.mult)
            scatter(t, h, 0, S)

        def third_copy(t, tag=None):
            strength = tile([P, S], F32, "strength%d" % t, tag)
            nc.scalar.copy(strength[:], third_sum(t)[:])
            return strength

        def put(t, saturating, periodic, strength, j0=0, j1=S):
            blocks = (j1 - j0) // P
            total = ps.tile([P, S], F32, name="total", tag="bank_b", bufs=1)
            for i, part in enumerate((saturating, periodic)):
                for b in range(blocks):
                    nc.tensor.matmul(total[:, P * b:P * (b + 1)], part[:, b, :], ident[:], is_transpose=True,
                                     start=(i == 0 and b == 0), stop=(i == 1 and b == blocks - 1))
            h = placed([P, S], F32, "h3", TAIL + 5120) if t == 3 else tile([P, S], F32, "h2")
            nc.vector.tensor_tensor(h[:], total[:, 0:j1 - j0], strength[:, j0:j1], ALU.mult)
            return h

        x1_moved = tile([P, 2, NP], BF16, "x1_moved")

        def move(queue, dst, src, t):
            for e in range(2):
                queue.dma_start(out=dst[64 * t:64 * t + 64, e, :], in_=src[e:P:2, :])

        def flux_pick(t, c0, c1, tag=None):
            picked = tile([P, c1 - c0], F32, "picked%d_%d" % (t, c0), tag)
            nc.vector.tensor_copy(picked[:], page[t][:].indirect(lists[3][:, c0 // 16:c1 // 16]))
            return picked

        def flux_scale(t, picked, dst, size):
            nc.scalar.activation(size[:], picked[:], ACT.Abs)
            for part, lo, hi in dst:
                nc.scalar.activation(part, size[:, lo:hi], ACT.Copy, scale=gain_col[t])

        def steel_pick(t, plane):
            nc.vector.tensor_copy(plane[:], page[t][:].indirect(lists[2][:]))
            move(nc.sync, x1_moved, plane, t)

        def flux_move(t, picked, size):
            plane = tile([P, NP], BF16, "plane2_%d" % t)
            flux_scale(t, picked, [(plane[:], 0, NP)], size)
            move(nc.scalar, x2_moved, plane, t)

        x2_moved = placed([P, 2, NP], BF16, "x2_moved", TAIL + 3072)
        RUN = PASSES * 4 * P
        stage1 = tile([P, 4 * RUN], BF16, "stage1")
        by_load = stage1[:].rearrange("p (o h a c) -> p h a o c", o=2, h=2, a=PASSES)
        for a in range(PASSES):
            cast_load(0, a, 0, by_load[:, 0, a])
            quantise_pass(0, a, 0, 0, stage1[:, 4 * P * a:4 * P * (a + 1)])
        for a in range(PASSES):
            stage = tile([P, 4 * P], BF16, "even1%d0" % a)
            cast_parity(nc.vector.tensor_copy, 1, a, 0, 0, stage[:])
            quantise_pass(1, a, 0, 0, stage[:])
        deal_w4(0, "raw000")
        saturating = tile([P, S], F32, "tanh0")
        nc.scalar.activation(saturating[:], direct_sum(0, 0, 0, S), ACT.Tanh)
        third = third_sum(0)
        put_direct(0, saturating, third)
        for i in range(2):
            w_s[i, 1, 0] = placed([P, PASSES * P], U8, "w_s%d1" % i, HOLD + 2048 + 256 * i)
        stage2 = tile([P, 3 * RUN], BF16, "stage2", "sin0")
        for a in range(PASSES):
            cast_parity(nc.scalar.copy, 1, a, 0, 1, stage2[:, 2 * RUN + 4 * P * a:2 * RUN + 4 * P * (a + 1)])
        for a in range(PASSES):
            cast_load(0, a, 1, by_load[:, 1, a])
        quantise(w_c[0, 1, 0][:], w_s[0, 1, 0][:], stage1[:, RUN:2 * RUN])
        picked0 = flux_pick(0, 0, NP, "raw011")
        cast_load(1, 0, 1, stage2[:, 0:2 * RUN].rearrange("p (o a c) -> p a o c", o=2, a=PASSES)[:, 0])
        steel_pick(0, tile([P, NP], BF16, "plane1_0", "raw101"))
        quantise_pass(1, 0, 1, 0, stage2[:, 0:4 * P])
        for o in range(2):
            cast_parity(nc.scalar.copy, 1, 1, 1, o, stage2[:, RUN * o + 4 * P:RUN * (o + 1)])
        quantise_pass(1, 1, 1, 0, stage2[:, 4 * P:RUN])
        late = placed([P, LATE // 4], F32, "late", 0)
        saturating = late[:, 0:S]
        odd_parts = [late[:, (1 + 2 * i) * S:(3 + 2 * i) * S].rearrange("p (b u r) -> p b u r", b=4, u=2) for i in range(2)]
        nc.scalar.activation(saturating, direct_sum(0, 1, 0, S), ACT.Tanh)
        quantise_odd(0, stage1[:, 2 * RUN:4 * RUN], (0, 1))
        quantise_odd(1, stage2[:, RUN:3 * RUN], (1, 0))
        put_direct(1, saturating, third_sum(1))
        deal_w4(1, "raw010")
        picked1 = flux_pick(1, 0, NP)
        steel_pick(1, tile([P, NP], BF16, "plane1_1"))
        strength = third_copy(2, "sin1")
        flux_move(0, picked0, tile([P, NP], F32, "size0", "sum1"))
        for i in range(2):
            for hf in range(2):
                transposed_part(i, hf, 1, odd_parts[i][:, :, :, 64 * hf:64 * (hf + 1)])
        scatter(2, put(2, odd_parts[0][:, :, 0, :], odd_parts[1][:, :, 0, :], strength), 0, S)
        flux_move(1, picked1, placed([P, NP], F32, "size1", HOLD + 2560))
        x2_g = [placed([P, 256, 4], BF16, "x2_g0", TAIL), tile([P, 256, 4], BF16, "x2_g1")]
        h = put(3, odd_parts[0][:, :, 1, :], odd_parts[1][:, :, 1, :], third_copy(3))
        spread = ps.tile([P, 4, P], F32, name="spread", tag="bank_a", bufs=1)
        for b in range(4):
            nc.tensor.matmul(spread[:, b, :], flux_cols[:, b:b + 1].to_broadcast([P, P]), ident[:],
                             is_transpose=True, start=True, stop=True)
        flux_rows = tile([P, NP], F32, "flux_rows")
        nc.scalar.copy(flux_rows[:].rearrange("m (p b) -> m p b", b=4), spread[:].rearrange("m b p -> m p b"))
        picked2 = placed([P, NP], F32, "picked2", 0)
        nc.vector.tensor_copy(picked2[:], page[2][:].indirect(lists[3][:]))
        scatter(3, h, 0, S)
        picked3 = [flux_pick(3, 256 * c, 256 * (c + 1)) for c in range(2)]
        for c in range(2):
            nc.scalar.copy(x2_g[c][:, :, 0:2], x2_moved[:, :, 256 * c:256 * (c + 1)].rearrange("p e j -> p j e"))
        flux_scale(2, picked2, [(x2_g[c][:, :, 2], 256 * c, 256 * (c + 1)) for c in range(2)],
                   placed([P, NP], F32, "size2", TAIL + 3072))
        pieces = [(0, 256), (256, 512)]
        x1_g = []

        def steels_moved(n, offset):
            m0, m1 = pieces[n]
            x1_g.append(placed([P, m1 - m0, 4], BF16, "x1_g%d" % n, offset))
            nc.scalar.copy(x1_g[n][:, :, 0:2], x1_moved[:, :, m0:m1].rearrange("p e m -> p m e"))

        steels_moved(0, TAIL + 4096)
        size = placed([P, NP], F32, "size3", TAIL + 2048)
        for c in range(2):
            cols = slice(256 * c, 256 * (c + 1))
            nc.scalar.activation(size[:, cols], picked3[c][:], ACT.Abs)
            nc.scalar.activation(x2_g[c][:, :, 3], size[:, cols], ACT.Copy, scale=gain_col[3])

        x2_c = tile([P, NP], U32, "x2_c")
        x2_s = tile([P, NP], U8, "x2_s")
        x1_c = tile([P, NP], U32, "x1_c")
        x1_s = tile([P, NP], U8, "x1_s")

        def steels(n):
            m0, m1 = pieces[n]
            for t in (2, 3):
                nc.vector.tensor_copy(x1_g[n][:, :, t], page[t][:].indirect(lists[2][:, m0 // 16:m1 // 16]))
            quantise(x1_c[:, m0:m1], x1_s[:, m0:m1], x1_g[n][:].rearrange("p m s -> p (m s)"))

        def score(q):
            cols = slice(P * q, P * (q + 1))
            bank = ps.tile([P, NP], F32, name="score", tag="pre", bufs=4)
            for c in range(2):
                half = slice(256 * c, 256 * (c + 1))
                nc.tensor.matmul_mx(
                    out=bank[:, half], lhsT=x1_c[:, cols].bitcast(FP8X4), lhsT_scale=x1_s[:, cols],
                    rhs=x2_c[:, half].bitcast(FP8X4), rhs_scale=x2_s[:, half], start=True, stop=True)
            res = tile([P, NP], F32, "res%d" % q)
            nc.vector.tensor_tensor(res[:], bank[:], flux_rows[:], ALU.add)
            nc.sync.dma_start(out=out[cols, :], in_=res[:])

        def flux_quantise(c):
            cols = slice(256 * c, 256 * (c + 1))
            quantise(x2_c[:, cols], x2_s[:, cols], x2_g[c][:].rearrange("p j s -> p (j s)"))

        steels(0)
        for c in range(2):
            flux_quantise(c)
        steels_moved(1, TAIL)
        steels(1)
        for q in range(4):
            score(q)
